import numpy as np
import ml_dtypes


def mxq(x, axis, fmt="e4m3"):
    dtype, down = {"e4m3": (ml_dtypes.float8_e4m3fn, 7), "e5m2": (ml_dtypes.float8_e5m2, 14)}[fmt]
    v = np.moveaxis(np.asarray(x, np.float32).astype(ml_dtypes.bfloat16).astype(np.float64), axis, -1)
    blocks = v.reshape(v.shape[:-1] + (-1, 32))
    amax = np.abs(blocks).max(-1, keepdims=True)
    byte = np.maximum(np.where(amax > 0, np.frexp(amax)[1] - 1 + 127, 0) - down, 1)
    scale = np.exp2(byte - 127.0)
    codes = (blocks / scale).astype(np.float32).astype(dtype).astype(np.float64)
    return np.moveaxis((codes * scale).reshape(v.shape), -1, axis)


WIDE = False


def mx_kscale(k):
    if not WIDE:
        return np.ones(k)
    levels = np.array([10, -10, 5, -5, 0])
    if k % 512:
        return np.exp2(np.random.permutation(np.resize(levels, k // 32))).repeat(32)
    a = np.empty((k // 512, 16))
    for p in range(k // 512):
        a[p, :8] = np.random.permutation(np.resize(levels, 8))
        for g in range(8):
            far = levels[np.abs(levels - a[p, g]) >= 10]
            a[p, g + 8] = far[np.random.randint(len(far))]
    return np.exp2(a.ravel()).repeat(32)


def f64(x):
    return np.asarray(x).astype(np.float64)


def striped(idx):
    return np.tile(idx.reshape(-1, 16).T, (8, 1)).astype(np.uint16)


def unstriped(offs):
    return offs[:16].T.reshape(-1).astype(np.int64)


def striped8(idx):
    return np.concatenate([x.reshape(-1, 16).T for x in idx]).astype(np.uint16)


def runs(offs, k):
    lists = np.stack([offs[16 * r : 16 * r + 16].T.reshape(-1) for r in range(8)]).astype(np.int64)
    return lists[np.arange(k) % 512 // 64]


def pack_weight(w):
    k, n = w.shape
    w = f64(np.asarray(w, np.float32).astype(ml_dtypes.bfloat16)).reshape(k // 32, 32, n)
    amax = np.abs(w).max(1)
    byte = np.clip(np.where(amax > 0, np.frexp(amax)[1] - 1 + 127 - 7, 1), 1, 254)
    scaled = (w * np.exp2(127.0 - byte)[:, None, :]).reshape(k, n).astype(np.float32)
    words = np.ascontiguousarray(scaled.reshape(k // 512, 128, 4, n).transpose(0, 1, 3, 2)).astype(ml_dtypes.float8_e4m3fn).view(np.uint8)
    return words, np.ascontiguousarray(byte.astype(np.uint8).reshape(k // 512, 16, n))


def unpack_weight(words, scales):
    g, p, n, _ = words.shape
    vals = np.ascontiguousarray(words).view(ml_dtypes.float8_e4m3fn).astype(np.float64) * np.repeat(np.exp2(scales.astype(np.float64) - 127.0), 8, axis=1)[..., None]
    return vals.transpose(0, 1, 3, 2).reshape(g * 512, n)


def sigmoid(v):
    return 1.0 / (1.0 + np.exp(-np.maximum(v, -700.0)))


K, T, S, H, W, C = 512, 2048, 512, 512, 256, 512


def setup_inputs():
    n = np.random.standard_normal
    s = mx_kscale(K)[:, None]
    packed_xT = pack_weight(n((K, T)) * s)
    perm = np.stack([np.random.permutation(S) for _ in range(8)])
    return {
        "x_words": packed_xT[0],
        "x_scales": packed_xT[1],
        "w1": (n((K, H)) / np.sqrt(K) / s).astype(np.float32),
        "gs": (np.random.uniform(0.5, 1.5, (K, 1)) / s).astype(np.float32),
        "offs": striped(np.random.permutation(T)[:S]),
        "n1": striped8(perm[:, :W]),
        "n2": striped8(perm[:, W:]),
        "n3": striped8(np.stack([np.random.permutation(S) for _ in range(8)])),
        "ca": striped(np.random.permutation(T)[:C]),
        "cb": striped(np.random.permutation(T)[:C]),
        "n4": striped8(np.stack([np.random.permutation(S) for _ in range(8)])),
        "n5": striped8(np.stack([np.random.permutation(S) for _ in range(8)])),
    }


def reference(x_words, x_scales, w1, gs, offs, n1, n2, n3, ca, cb, n4, n5):
    x_ca = unpack_weight(x_words, x_scales)[:, unstriped(ca)]
    xq = unpack_weight(x_words, x_scales)[:, unstriped(offs)]
    y = mxq(f64(w1), 0, "e4m3").T @ xq
    pa = y[np.arange(H)[:, None], runs(n1, H)]
    pb = y[np.arange(H)[:, None], runs(n2, H)]
    ra = pa - (0.5 * pb)
    ds = y.copy()
    ds[np.arange(H)[:, None], runs(n2, H)] = ra
    z = f64(gs) * (ds - (0.5 * (ds[np.arange(H)[:, None], runs(n3, H)])))
    zq = mxq(z, 0, "e4m3")
    a = 0.0625 * (x_ca.T @ zq)
    x_cb = unpack_weight(x_words, x_scales)[:, unstriped(cb)]
    b = 0.0625 * (x_cb.T @ zq)
    return (a + a[np.arange(C)[:, None], runs(n4, C)]) * (sigmoid(b + b[np.arange(C)[:, None], runs(n5, C)]))

from contextlib import ExitStack

import concourse.mybir as mybir

K, T, S, H, W, C = 512, 2048, 512, 512, 256, 512
FLOPS = 3 * 2 * 512 * 512 * 512

F32 = mybir.dt.float32
BF16 = mybir.dt.bfloat16
I32 = mybir.dt.int32
U32 = mybir.dt.uint32
U16 = mybir.dt.uint16
U8 = mybir.dt.uint8
FP8X4 = mybir.dt.float8_e4m3fn_x4
ADD = mybir.AluOpType.add
MULT = mybir.AluOpType.mult
COPY = mybir.ActivationFunctionType.Copy
SIGMOID = mybir.ActivationFunctionType.Sigmoid

P = 128
PACK = 4
HALF = 256
Z_CHUNKS = ((0, 256), (256, 384), (384, 512))


def entries(list_tile, lo, hi):
    return list_tile[:, lo // 16 : hi // 16]


def tile_picked_ccmptriebfoldd_none_p_kernel(
    tc, x_words, x_scales, w1, gs, offs, n1, n2, n3, ca, cb, n4, n5, out
):
    nc = tc.nc
    with ExitStack() as ctx:
        keep = ctx.enter_context(tc.tile_pool(name="keep", bufs=1))
        psum = ctx.enter_context(tc.psum_pool(name="psum", bufs=8))

        def load_list(src, name):
            tile = keep.tile(list(src.shape), U16, name=name)
            nc.sync.dma_start(tile[:], src)
            return tile

        def row_tiles(name, width):
            return [keep.tile([P, width], F32, name=f"{name}{t}", tag=f"{name}{t}", align_bytes=64) for t in range(PACK)]

        def product(lhs_words, lhs_bytes, rhs_words, rhs_bytes, acc):
            nc.tensor.matmul_mx(
                out=acc,
                lhsT=lhs_words.bitcast(FP8X4),
                lhsT_scale=lhs_bytes,
                rhs=rhs_words.bitcast(FP8X4),
                rhs_scale=rhs_bytes,
                start=True,
                stop=True,
            )

        table_bytes = keep.tile([P, T], U8, align_bytes=64)
        nc.vector.memset(table_bytes[:].bitcast(I32), 0)
        warm_in = keep.tile([P, 1], F32)
        warm_out = keep.tile([P, 1], F32)
        nc.gpsimd.memset(warm_in[:], 0.0)
        offs_t = load_list(offs, "offs_t")
        cb_t = load_list(cb, "cb_t")
        ca_t = load_list(ca, "ca_t")
        for q in range(4):
            nc.sync.dma_start(
                table_bytes[32 * q : 32 * q + 4, :].bitcast(I32),
                x_scales[0, 4 * q : 4 * q + 4, :].bitcast(I32),
            )
        nc.scalar.activation(warm_out[:], warm_in[:], SIGMOID)
        w_rows = w1.rearrange("(p j) c -> p j c", j=PACK)
        w_raw = [keep.tile([P, PACK, HALF], F32, name=f"w_raw{h}", align_bytes=64) for h in range(2)]
        for h in range(2):
            nc.sync.dma_start(w_raw[h][:], w_rows[:, :, h * HALF : (h + 1) * HALF])
        table_words = keep.tile([P, T], U32, align_bytes=64)
        nc.sync.dma_start(table_words[:].bitcast(I32), x_words[0].rearrange("p n r -> p (n r)").bitcast(I32))
        gain = keep.tile([P, PACK], F32)
        nc.sync.dma_start(gain[:], gs.rearrange("(p t) o -> p (t o)", t=PACK))
        n1_t = load_list(n1, "n1_t")
        n2_t = load_list(n2, "n2_t")
        n3_t = load_list(n3, "n3_t")
        n5_t = load_list(n5, "n5_t")
        n4_t = load_list(n4, "n4_t")

        x_bytes = keep.tile([P, S], U8, align_bytes=64)
        nc.vector.tensor_copy(x_bytes[:], table_bytes[:].indirect(offs_t[:]))
        pair_bytes_raw = keep.tile([P, 2, C], U8, align_bytes=64)
        nc.vector.tensor_copy(pair_bytes_raw[:, 0, :], table_bytes[:].indirect(cb_t[:]))
        nc.vector.tensor_copy(pair_bytes_raw[:, 1, :], table_bytes[:].indirect(ca_t[:]))
        pair_bytes = keep.tile([P, 2, PACK, P], U8, align_bytes=64)
        nc.vector.tensor_copy(pair_bytes[:], pair_bytes_raw[:].rearrange("p l (m t) -> p l t m", t=PACK))

        w_bf = keep.tile([P, PACK, P, PACK], BF16, align_bytes=64)
        for h in range(2):
            nc.scalar.copy(
                w_bf[:, :, h * 64 : (h + 1) * 64, :].rearrange("p t m j -> p m j t"),
                w_raw[h][:].rearrange("p j (m t) -> p m j t", t=PACK),
            )
        w_words = keep.tile([P, H], U32, align_bytes=64)
        w_bytes = keep.tile([P, H], U8, align_bytes=64)
        nc.vector.quantize_mx(
            out=w_words[:].bitcast(FP8X4), scales=w_bytes[:], in_=w_bf[:].rearrange("p t m j -> p (t m j)")
        )

        x_picked = keep.tile([P, S], U32, align_bytes=64)
        nc.vector.tensor_copy(x_picked[:], table_words[:].indirect(offs_t[:]))
        cb_words = keep.tile([P, C], U32, align_bytes=64)
        nc.vector.tensor_copy(cb_words[:].rearrange("p (t m) -> p m t", t=PACK), table_words[:].indirect(cb_t[:]))

        ds = row_tiles("ds", S)
        for t in range(PACK):
            cols = slice(t * P, (t + 1) * P)
            acc = psum.tile([P, S], F32, name="acc")
            product(w_words[:, cols], w_bytes[:, cols], x_picked[:], x_bytes[:], acc[:])
            nc.scalar.activation(ds[t][:], acc[:], COPY, scale=gain[:, t : t + 1])

        pa = row_tiles("pa", W)
        pb = row_tiles("pb", W)
        half_ds = row_tiles("half_ds", S)

        def fetch_pairs(t):
            nc.vector.tensor_copy(pa[t][:], ds[t][:].indirect(n1_t[:]))
            nc.vector.tensor_scalar(pb[t][:], ds[t][:].indirect(n2_t[:]), -0.5, 0.0, MULT, ADD)

        def put_back(t):
            nc.vector.tensor_tensor(ds[t][:].indirect(n2_t[:]), pa[t][:], pb[t][:], ADD)
            nc.scalar.activation(half_ds[t][:], ds[t][:], COPY, scale=-0.5)

        fetch_pairs(0)
        for t in range(1, PACK):
            fetch_pairs(t)
            put_back(t - 1)
        put_back(PACK - 1)

        z_words = keep.tile([P, S], U32, align_bytes=64)
        z_bytes = keep.tile([P, S], U8, align_bytes=64)
        z_bf = []
        for c, (lo, hi) in enumerate(Z_CHUNKS):
            z32 = keep.tile([P, PACK, hi - lo], F32, name=f"z32_{c}", align_bytes=64)
            for t in range(PACK):
                nc.vector.tensor_tensor(
                    z32[:, t, :], half_ds[t][:].indirect(entries(n3_t, lo, hi)), ds[t][:, lo:hi], ADD
                )
            zb = keep.tile([P, hi - lo, PACK], BF16, name=f"z_bf{c}", align_bytes=64)
            nc.scalar.copy(
                zb[:].rearrange("p (c i) t -> p c t i", i=4), z32[:].rearrange("p t (c i) -> p c t i", i=4)
            )
            z_bf.append(zb)

        def quantise_z(c):
            lo, hi = Z_CHUNKS[c]
            nc.vector.quantize_mx(
                out=z_words[:, lo:hi].bitcast(FP8X4),
                scales=z_bytes[:, lo:hi],
                in_=z_bf[c][:].rearrange("p s t -> p (s t)"),
            )

        b_win = row_tiles("b_win", S)
        b_own = row_tiles("b_own", S)
        a_win = row_tiles("a_win", S)
        a_own = row_tiles("a_own", S)

        def leave_bank(acc, win, own, lo, hi):
            nc.scalar.activation(win[:, lo:hi], acc, COPY, scale=0.0625)
            nc.scalar.activation(own[:, lo:hi], acc, COPY, scale=0.0625)

        early = Z_CHUNKS[-1][0]
        acc_early = psum.tile([P, S], F32, name="acc")
        for c in range(len(Z_CHUNKS) - 1):
            lo, hi = Z_CHUNKS[c]
            quantise_z(c)
            product(cb_words[:, 0:P], pair_bytes[:, 0, 0, :], z_words[:, lo:hi], z_bytes[:, lo:hi], acc_early[:, lo:hi])
        leave_bank(acc_early[:, 0:early], b_win[0], b_own[0], 0, early)

        ca_words = keep.tile([P, C], U32, name="ca_words", tag="half_ds3", align_bytes=64)
        nc.vector.tensor_copy(ca_words[:].rearrange("p (t m) -> p m t", t=PACK), table_words[:].indirect(ca_t[:]))

        quantise_z(len(Z_CHUNKS) - 1)
        acc_late = psum.tile([P, S], F32, name="acc")
        product(cb_words[:, 0:P], pair_bytes[:, 0, 0, :], z_words[:, early:S], z_bytes[:, early:S], acc_late[:, early:S])
        leave_bank(acc_late[:, early:S], b_win[0], b_own[0], early, S)

        def scores(words, which, t, win, own):
            acc = psum.tile([P, S], F32, name="acc")
            product(words[:, t * P : (t + 1) * P], pair_bytes[:, which, t, :], z_words[:], z_bytes[:], acc[:])
            leave_bank(acc[:], win[t], own[t], 0, S)

        b_sum = row_tiles("b_sum", S)
        a_sum = row_tiles("a_sum", S)
        gate = row_tiles("gate", S)
        result = row_tiles("result", S)
        out_rows = out.rearrange("(p t) s -> t p s", t=PACK)

        def add_partner(total, win, own, places):
            for lo in range(0, S, HALF):
                hi = lo + HALF
                nc.vector.tensor_tensor(total[:, lo:hi], win[:].indirect(entries(places, lo, hi)), own[:, lo:hi], ADD)

        def finish(t, lo, hi):
            nc.vector.tensor_tensor(result[t][:, lo:hi], a_sum[t][:, lo:hi], gate[t][:, lo:hi], MULT)
            nc.sync.dma_start(out_rows[t][:, lo:hi], result[t][:, lo:hi])

        add_partner(b_sum[0], b_win[0], b_own[0], n5_t)
        for t in range(PACK):
            scores(ca_words, 1, t, a_win, a_own)
            if t + 1 < PACK:
                scores(cb_words, 0, t + 1, b_win, b_own)
            nc.scalar.activation(gate[t][:], b_sum[t][:], SIGMOID)
            add_partner(a_sum[t], a_win[t], a_own[t], n4_t)
            if t + 1 < PACK:
                add_partner(b_sum[t + 1], b_win[t + 1], b_own[t + 1], n5_t)
                finish(t, 0, S)
            else:
                finish(t, 0, HALF)
                finish(t, HALF, S)
